import numpy as np
import ml_dtypes


def mxq(x, axis, fmt="e4m3"):
    dtype, down = {"e4m3": (ml_dtypes.float8_e4m3fn, 7), "e5m2": (ml_dtypes.float8_e5m2, 14)}[fmt]
    v = np.moveaxis(np.asarray(x, np.float32).astype(ml_dtypes.bfloat16).astype(np.float64), axis, -1)
    blocks = v.reshape(v.shape[:-1] + (-1, 32))
    amax = np.abs(blocks).max(-1, keepdims=True)
    byte = np.maximum(np.where(amax > 0, np.frexp(amax)[1] - 1 + 127, 0) - down, 1)
    scale = np.exp2(byte - 127.0)
    codes = (blocks / scale).astype(np.float32).astype(dtype).astype(np.float64)
    return np.moveaxis((codes * scale).reshape(v.shape), -1, axis)


WIDE = False


def mx_kscale(k):
    if not WIDE:
        return np.ones(k)
    levels = np.array([10, -10, 5, -5, 0])
    if k % 512:
        return np.exp2(np.random.permutation(np.resize(levels, k // 32))).repeat(32)
    a = np.empty((k // 512, 16))
    for p in range(k // 512):
        a[p, :8] = np.random.permutation(np.resize(levels, 8))
        for g in range(8):
            far = levels[np.abs(levels - a[p, g]) >= 10]
            a[p, g + 8] = far[np.random.randint(len(far))]
    return np.exp2(a.ravel()).repeat(32)


BF16 = ml_dtypes.bfloat16


def bf(x):
    return np.asarray(x, np.float32).astype(BF16)


def f64(x):
    return np.asarray(x).astype(np.float64)

def planes(Y):
    n, m = Y.shape
    b = f64(bf(Y)).reshape(n // 32, 32, m)
    amax = np.abs(b).max(1)
    byte = np.clip(np.where(amax > 0, np.frexp(amax)[1] - 1 + 127 - 7, 1), 1, 254)
    codes = (b * np.exp2(127.0 - byte)[:, None, :]).reshape(n, m).astype(np.float32).astype(ml_dtypes.float8_e4m3fn).view(np.uint8)
    words = codes.reshape(n // 512, 128, 4, m).transpose(0, 1, 3, 2)
    return np.ascontiguousarray(words), np.ascontiguousarray(byte.astype(np.uint8).reshape(n // 512, 16, m))


T, N, M, Q = 1024, 4, 256, 128
D = N * M
R = N * Q


def kron_sum(a, v):
    n, rows_a, cols_a = a.shape
    _, rows_v, cols_v = v.shape
    total = a[0][:, None, :, None] * v[0][None, :, None, :]
    for i in range(1, n):
        total = total + a[i][:, None, :, None] * v[i][None, :, None, :]
    return total.reshape(rows_a * rows_v, cols_a * cols_v)


def erf(z):
    c = np.clip(z, -6.0, 6.0)
    c2 = 2.0 * c * c
    term = c
    total = c
    for n in range(1, 151):
        term = term * c2 / (2 * n + 1)
        total = total + term
    return np.where(np.abs(z) >= 6.0, np.sign(z), 2.0 / np.sqrt(np.pi) * np.exp(-c * c) * total)


def gelu_erf(z):
    return 0.5 * z * (1.0 + erf(z / np.sqrt(2.0)))


def setup_inputs():
    s, t = mx_kscale(D), mx_kscale(R)
    sign = np.where(np.random.standard_normal((N, N, N)) < 0.0, -1.0, 1.0)
    return {
        "x": bf(np.random.standard_normal((T, D)) * s),
        "a": bf(sign * np.random.uniform(0.6, 1.4, (N, N, N)) / np.sqrt(N)),
        "v1": bf(np.random.standard_normal((N, M, Q)) / np.sqrt(D)),
        "v2": bf(1.5 * np.random.standard_normal((N, Q, M)) / np.sqrt(R)),
        "g_down": bf((1.0 + 0.1 * np.random.standard_normal(D)) / s),
        "g_mid": bf((1.0 + 0.1 * np.random.standard_normal(R)) * t),
        "g_up": bf((1.0 + 0.1 * np.random.standard_normal(R)) / t),
    }


def core(x, a, v1, v2, g_down, g_mid, g_up):
    w_down = f64(g_down)[:, None] * kron_sum(f64(a), f64(v1))
    w_up = f64(g_up)[:, None] * kron_sum(f64(a), f64(v2))
    h = mxq(f64(x), 1, "e4m3") @ mxq(w_down, 0, "e4m3")
    u = gelu_erf(h) * f64(g_mid)[None, :]
    return mxq(u, 1, "e4m3") @ mxq(w_up, 0, "e4m3")


def reference(x, a, v1, v2, g_down, g_mid, g_up):
    R_out = core(x, a, v1, v2, g_down, g_mid, g_up)
    words, scales = planes(R_out)
    return R_out, words, scales

@@ -1,0 +1,436 @@
+from contextlib import ExitStack
+
+import concourse.mybir as mybir
+from concourse.masks import make_identity
+
+FLOPS = 2 * 1024 * 1024 * 512 * 2
+
+F32 = mybir.dt.float32
+BF16 = mybir.dt.bfloat16
+U32 = mybir.dt.uint32
+I32 = mybir.dt.int32
+U8 = mybir.dt.uint8
+FP8 = mybir.dt.float8_e4m3fn_x4
+ACT = mybir.ActivationFunctionType
+ALU = mybir.AluOpType
+
+P = 128
+NV1 = 4
+NV2 = 8
+
+
+def tile_compacterhypercomplexadapter_x1_kernel(
+    tc, x, a, v1, v2, g_down, g_mid, g_up, out_0, out_1, out_2
+):
+    nc = tc.nc
+    with ExitStack() as ctx:
+        keep = ctx.enter_context(tc.tile_pool(name="keep", bufs=1))
+        work = ctx.enter_context(tc.tile_pool(name="work", bufs=2))
+        psum = ctx.enter_context(tc.psum_pool(name="psum", bufs=8))
+        ctx.enter_context(tc.manual_schedule())
+
+        v1_raw = keep.tile([P, 4, 2, 128], BF16, name="v1_raw", align_bytes=64)
+        nc.sync.dma_start(out=v1_raw[:], in_=v1.rearrange("i (j h) q -> j i h q", h=2))
+        v2_raw = keep.tile([P, 4, 256], BF16, name="v2_raw", align_bytes=64)
+        nc.sync.dma_start(out=v2_raw[:], in_=v2.rearrange("i q m -> q i m"))
+        a_bf = keep.tile([P, 64], BF16, name="a_bf", align_bytes=64)
+        nc.scalar.dma_start(out=a_bf[:], in_=a.rearrange("i r c -> (i r c)").partition_broadcast(P))
+        gd = keep.tile([P, 2, 4], BF16, name="gd", align_bytes=64)
+        nc.scalar.dma_start(out=gd[:], in_=g_down.rearrange("(g p t) -> p g t", g=2, t=4))
+        gu = keep.tile([P, 4], BF16, name="gu", align_bytes=64)
+        nc.scalar.dma_start(out=gu[:], in_=g_up.rearrange("(p t) -> p t", t=4))
+        gm = keep.tile([P, 4], BF16, name="gm", align_bytes=64)
+        nc.scalar.dma_start(out=gm[:], in_=g_mid.rearrange("(p t) -> p t", t=4))
+        x_raw = {}
+        for h in range(2):
+            xv = x[512 * h : 512 * h + 512, :].rearrange("(p t) k -> p t k", t=4)
+            for tp in range(2):
+                xt = keep.tile([P, 2, 1024], BF16, name="x_raw_%d%d" % (h, tp), align_bytes=64)
+                nc.sync.dma_start(out=xt[:], in_=xv[:, 2 * tp : 2 * tp + 2, :])
+                x_raw[h, tp] = xt
+
+        id32 = keep.tile([P, 128], F32, name="id32", align_bytes=64)
+        make_identity(nc, id32[:])
+        id16 = keep.tile([P, 128], BF16, name="id16", align_bytes=64)
+        make_identity(nc, id16[:])
+
+        warm = keep.tile([P, 2], F32, name="warm", align_bytes=64)
+        nc.vector.memset(warm[:], 0.0)
+        nc.scalar.activation(out=warm[:, 0:1], in_=warm[:, 1:2], func=ACT.Gelu)
+        a32 = keep.tile([P, 64], F32, name="a32", align_bytes=64)
+        nc.vector.tensor_copy(out=a32[:], in_=a_bf[:])
+
+        def bank(name, dtype=F32, shape=(P, 512)):
+            return psum.tile(list(shape), dtype, name=name, tag="bank")
+
+        def product(engine, out, in_, i, r, c):
+            s = i * 16 + r * 4 + c
+            if engine == 0:
+                nc.vector.tensor_scalar(out=out, in0=in_, scalar1=a32[:, s : s + 1], scalar2=None, op0=ALU.mult)
+            else:
+                nc.scalar.activation(out=out, in_=in_, func=ACT.Copy, scale=a32[:, s : s + 1])
+
+        v1T = keep.tile([P, 4, 2, 128], BF16, name="v1T", align_bytes=64)
+        v2T = keep.tile([P, 4, 2, 128], BF16, name="v2T", align_bytes=64)
+
+        def turn_v1():
+            for k in range(2):
+                b = bank("vb", BF16, (P, 2, 2, 128))
+                for i in range(2):
+                    for h in range(2):
+                        nc.tensor.transpose(b[:, i, h, :], v1_raw[:, 2 * k + i, h, :], id16[:])
+                if k == 0:
+                    nc.scalar.copy(out=v1T[:, 0:2], in_=b[:])
+                else:
+                    nc.vector.tensor_copy(out=v1T[:, 2:4], in_=b[:])
+
+        def turn_v2():
+            for k in range(2):
+                b = bank("vb", BF16, (P, 2, 2, 128))
+                for i in range(2):
+                    for h in range(2):
+                        nc.tensor.transpose(b[:, i, h, :], v2_raw[:, 2 * k + i, 128 * h : 128 * h + 128], id16[:])
+                if k == 0:
+                    nc.scalar.copy(out=v2T[:, 0:2], in_=b[:])
+                else:
+                    nc.vector.tensor_copy(out=v2T[:, 2:4], in_=b[:])
+
+        prods = {}
+        banks = {}
+
+        def prod1(u, nv):
+            g, c = divmod(u, 4)
+            pt = work.tile([P, 4, 4, 2, 64], F32, name="p1", bufs=3, align_bytes=64)
+            prods[1, u] = pt
+            for n in range(8):
+                i, rr = divmod(n, 2)
+                product(
+                    0 if n < nv else 1,
+                    pt[:, i, :, rr, :].rearrange("p (b h) w -> p b h w", h=2),
+                    v1T[:, i].rearrange("p h (w b) -> p b h w", b=2),
+                    i, 2 * g + rr, c,
+                )
+
+        def tr1(u):
+            pt = prods[1, u]
+            b = bank("u1", F32, (P, 4, 128))
+            banks[1, u] = b
+            for t in range(4):
+                for i in range(4):
+                    nc.tensor.matmul(
+                        out=b[:, t, :], lhsT=pt[:, i, t].rearrange("p r w -> p (r w)"), rhs=id32[:],
+                        start=(i == 0), stop=(i == 3), is_transpose=True,
+                    )
+
+        wd_bf = {}
+        wd_codes = {}
+        wd_scales = {}
+        for g in range(2):
+            wd_bf[g] = keep.tile([P, 4, 4, 32, 4], BF16, name="wd_bf%d" % g, align_bytes=64)
+            wd_codes[g] = keep.tile([P, 512], U32, name="wd_codes%d" % g, align_bytes=64)
+            wd_scales[g] = keep.tile([P, 512], U8, name="wd_scales%d" % g, align_bytes=64)
+
+        def ev1(u):
+            g, c = divmod(u, 4)
+            nc.vector.tensor_tensor(
+                out=wd_bf[g][:, :, c, :, :],
+                in0=banks[1, u][:].rearrange("p t (w s) -> p s w t", s=4),
+                in1=gd[:, g, :].unsqueeze(1).unsqueeze(1).to_broadcast([P, 4, 32, 4]),
+                op=ALU.mult,
+            )
+
+        def q_wd(g):
+            nc.vector.quantize_mx(
+                out=wd_codes[g][:].bitcast(FP8), scales=wd_scales[g][:],
+                in_=wd_bf[g][:].rearrange("p s c w t -> p (s c w t)"),
+            )
+
+        def prod2_tile(c):
+            prods[2, c] = work.tile([P, 2, 4, 4, 4, 32], F32, name="p2", bufs=3, align_bytes=64)
+
+        def prod2(c, engine, n0, n1):
+            pt = prods[2, c]
+            for n in range(n0, n1):
+                i, r = divmod(n, 4)
+                product(
+                    engine,
+                    pt[:, :, i, :, r, :],
+                    v2T[:, i].rearrange("p h (w t) -> p h t w", t=4),
+                    i, r, c,
+                )
+
+        def tr2(c, h):
+            pt = prods[2, c]
+            b = bank("u2", F32, (P, 4, 128))
+            banks[2, c, h] = b
+            for t in range(4):
+                for i in range(4):
+                    nc.tensor.matmul(
+                        out=b[:, t, :], lhsT=pt[:, h, i, t].rearrange("p r w -> p (r w)"), rhs=id32[:],
+                        start=(i == 0), stop=(i == 3), is_transpose=True,
+                    )
+
+        wu_bf = {}
+        wu_codes = {}
+        wu_scales = {}
+        for c in range(4):
+            wu_codes[c] = keep.tile([P, 256], U32, name="wu_codes%d" % c, align_bytes=64)
+            wu_scales[c] = keep.tile([P, 256], U8, name="wu_scales%d" % c, align_bytes=64)
+            wu_bf[c] = keep.tile([P, 256, 4], BF16, name="wu_bf%d" % c, align_bytes=64)
+
+        def ev2(c, h):
+            nc.vector.tensor_tensor(
+                out=wu_bf[c][:, 128 * h : 128 * h + 128, :],
+                in0=banks[2, c, h][:].rearrange("p t m -> p m t"),
+                in1=gu[:].unsqueeze(1).to_broadcast([P, 128, 4]),
+                op=ALU.mult,
+            )
+
+        def q_wu(c):
+            nc.vector.quantize_mx(
+                out=wu_codes[c][:].bitcast(FP8), scales=wu_scales[c][:],
+                in_=wu_bf[c][:].rearrange("p m t -> p (m t)"),
+            )
+
+        x_bf = {}
+        x_codes = {}
+        x_scales = {}
+        for h in range(2):
+            for g in range(2):
+                x_bf[h, g] = keep.tile([P, 512, 4], BF16, name="x_bf%d%d" % (h, g), align_bytes=64)
+                x_codes[h, g] = keep.tile([P, 512], U32, name="x_codes%d%d" % (h, g), align_bytes=64)
+                x_scales[h, g] = keep.tile([P, 512], U8, name="x_scales%d%d" % (h, g), align_bytes=64)
+
+        def x_turn(j):
+            h, tp, g = j // 4, (j // 2) % 2, j % 2
+            b = bank("xb", F32, (P, 2, 2, 128))
+            banks[0, j] = b
+            for k in range(2):
+                words = x_raw[h, tp][:, k, :].bitcast(F32)
+                for u in range(2):
+                    nc.tensor.transpose(b[:, k, u, :], words[:, 256 * g + u : 256 * (g + 1) : 2], id32[:])
+
+        def x_out(j, engine):
+            h, tp, g = j // 4, (j // 2) % 2, j % 2
+            dst = x_bf[h, g][:, 256 * tp : 256 * tp + 256, :].rearrange("p n t -> p (n t)").bitcast(F32)
+            (nc.vector.tensor_copy if engine == 0 else nc.scalar.copy)(
+                out=dst.rearrange("p (k r u) -> p k r u", k=2, u=2),
+                in_=banks[0, j][:].rearrange("p k u r -> p k r u"),
+            )
+
+        def q_x(h, g):
+            nc.vector.quantize_mx(
+                out=x_codes[h, g][:].bitcast(FP8), scales=x_scales[h, g][:],
+                in_=x_bf[h, g][:].rearrange("p n t -> p (n t)"),
+            )
+
+        hg = {}
+        u_bf = {}
+        u_codes = {}
+        u_scales = {}
+        for h in range(2):
+            hg[h] = keep.tile([P, 4, 512], F32, name="hg%d" % h, align_bytes=64)
+            u_codes[h] = keep.tile([P, 512], U32, name="u_codes%d" % h, align_bytes=64)
+            u_scales[h] = keep.tile([P, 512], U8, name="u_scales%d" % h, align_bytes=64)
+            for k in range(2):
+                u_bf[h, k] = keep.tile([P, 256, 4], BF16, name="u_bf%d%d" % (h, k), align_bytes=64)
+
+        def mm1(h, s):
+            b = bank("hb")
+            for g in range(2):
+                nc.tensor.matmul_mx(
+                    out=b[:],
+                    lhsT=wd_codes[g][:, 128 * s : 128 * s + 128].bitcast(FP8),
+                    lhsT_scale=wd_scales[g][:, 128 * s : 128 * s + 128],
+                    rhs=x_codes[h, g][:].bitcast(FP8), rhs_scale=x_scales[h, g][:],
+                    start=(g == 0), stop=(g == 1),
+                )
+            nc.scalar.activation(out=hg[h][:, s, :], in_=b[:], func=ACT.Gelu)
+
+        def u_mul(h, k):
+            nc.vector.tensor_tensor(
+                out=u_bf[h, k][:],
+                in0=hg[h][:, :, 256 * k : 256 * k + 256].rearrange("p s n -> p n s"),
+                in1=gm[:].unsqueeze(1).to_broadcast([P, 256, 4]),
+                op=ALU.mult,
+            )
+
+        def q_u(h, k):
+            nc.vector.quantize_mx(
+                out=u_codes[h][:, 256 * k : 256 * k + 256].bitcast(FP8),
+                scales=u_scales[h][:, 256 * k : 256 * k + 256],
+                in_=u_bf[h, k][:].rearrange("p n t -> p (n t)"),
+            )
+
+        of = {}
+        ob = {}
+
+        def mm2(h, c, e):
+            b = bank("ob", F32, (P, 2, 256))
+            banks[3, h, c, e] = b
+            for k in range(2):
+                t = 2 * e + k
+                nc.tensor.matmul_mx(
+                    out=b[:, k, :],
+                    lhsT=u_codes[h][:, 128 * t : 128 * t + 128].bitcast(FP8),
+                    lhsT_scale=u_scales[h][:, 128 * t : 128 * t + 128],
+                    rhs=wu_codes[c][:].bitcast(FP8), rhs_scale=wu_scales[c][:],
+                    start=True, stop=True,
+                )
+
+        def out_copy(h, c, e, engine):
+            if e == 0:
+                of[h, c] = work.tile([P, 4, 256], F32, name="of", bufs=4, align_bytes=64)
+            (nc.vector.tensor_copy if engine == 0 else nc.scalar.copy)(
+                out=of[h, c][:, 2 * e : 2 * e + 2, :], in_=banks[3, h, c, e][:]
+            )
+
+        def store_out(h, c):
+            nc.sync.dma_start(
+                out=out_0[512 * h : 512 * h + 512, 256 * c : 256 * c + 256].rearrange("(p t) n -> p t n", t=4),
+                in_=of[h, c][:],
+            )
+
+        def cast_out(h, c, engine):
+            ob[h, c] = work.tile([P, 256, 4], BF16, name="ob_bf", bufs=4, align_bytes=64)
+            (nc.vector.tensor_copy if engine == 0 else nc.scalar.copy)(
+                out=ob[h, c][:], in_=of[h, c][:].rearrange("p t n -> p n t")
+            )
+
+        oc = {}
+        osc = {}
+        for h in range(2):
+            osc[h] = keep.tile([P, 1024], U8, name="osc%d" % h, align_bytes=64)
+
+        def q_out(h, c):
+            cols = slice(256 * c, 256 * c + 256)
+            oc[h, c] = work.tile([P, 256], U32, name="oc", bufs=4, align_bytes=64)
+            nc.vector.quantize_mx(
+                out=oc[h, c][:].bitcast(FP8), scales=osc[h][:, cols], in_=ob[h, c][:].rearrange("p n t -> p (n t)")
+            )
+            nc.sync.dma_start(
+                out=out_1[h, :, cols, :].rearrange("p m t -> p (m t)").bitcast(I32), in_=oc[h, c][:].bitcast(I32)
+            )
+
+        def store_scales(h):
+            for qd in range(4):
+                nc.sync.dma_start(
+                    out=out_2[h, 4 * qd : 4 * qd + 4, :].bitcast(I32),
+                    in_=osc[h][32 * qd : 32 * qd + 4, :].bitcast(I32),
+                )
+
+        turn_v1()
+        turn_v2()
+        prod1(0, 4)
+        prod1(1, 4)
+        for u in range(8):
+            tr1(u)
+            if u in (2, 3, 4, 5):
+                x_turn(u - 2)
+            if u + 2 < 8:
+                prod1(u + 2, 4)
+            if u == 6:
+                prod2_tile(0)
+                prod2(0, 0, 0, 6)
+                prod2(0, 1, 6, 11)
+            if u == 7:
+                prod2(0, 1, 11, 16)
+            ev1(u)
+            if u in (2, 3, 4, 5):
+                x_out(u - 2, 1)
+            if u == 3:
+                q_wd(0)
+            if u == 4:
+                q_x(0, 0)
+            if u == 5:
+                q_x(0, 1)
+        prod2_tile(1)
+        tr2(0, 0)
+        q_wd(1)
+        prod2(1, 0, 0, 6)
+        prod2(1, 1, 6, 11)
+        tr2(0, 1)
+        ev2(0, 0)
+        for s in range(4):
+            mm1(0, s)
+        ev2(0, 1)
+        x_turn(4)
+        x_turn(5)
+        x_out(4, 0)
+        x_out(5, 0)
+        prod2(1, 1, 11, 16)
+        q_wu(0)
+        tr2(1, 0)
+        u_mul(0, 0)
+        u_mul(0, 1)
+        q_u(0, 0)
+        q_u(0, 1)
+        x_turn(6)
+        x_turn(7)
+        x_out(6, 1)
+        x_out(7, 1)
+        ev2(1, 0)
+        prod2_tile(2)
+        prod2(2, 0, 0, 6)
+        q_x(1, 0)
+        q_x(1, 1)
+        prod2(2, 1, 6, 16)
+        tr2(1, 1)
+        ev2(1, 1)
+        for e in range(2):
+            mm2(0, 0, e)
+            out_copy(0, 0, e, 1)
+        store_out(0, 0)
+        q_wu(1)
+        for s in range(4):
+            mm1(1, s)
+        cast_out(0, 0, 0)
+        tr2(2, 0)
+        q_out(0, 0)
+        prod2_tile(3)
+        prod2(3, 0, 0, 6)
+        u_mul(1, 0)
+        u_mul(1, 1)
+        for e in range(2):
+            mm2(0, 1, e)
+            out_copy(0, 1, e, 1)
+        store_out(0, 1)
+        q_u(1, 0)
+        q_u(1, 1)
+        tr2(2, 1)
+        prod2(3, 1, 6, 16)
+        ev2(2, 0)
+        cast_out(0, 1, 0)
+        ev2(2, 1)
+        q_out(0, 1)
+        for c in range(2):
+            for e in range(2):
+                mm2(1, c, e)
+                out_copy(1, c, e, 1)
+            store_out(1, c)
+        q_wu(2)
+        tr2(3, 0)
+        cast_out(1, 0, 0)
+        q_out(1, 0)
+        tr2(3, 1)
+        cast_out(1, 1, 0)
+        ev2(3, 0)
+        ev2(3, 1)
+        q_out(1, 1)
+        q_wu(3)
+        for h in range(2):
+            for e in range(2):
+                mm2(h, 2, e)
+                out_copy(h, 2, e, 1)
+            store_out(h, 2)
+            cast_out(h, 2, 0)
+            q_out(h, 2)
+        for h in range(2):
+            for e in range(2):
+                mm2(h, 3, e)
+                out_copy(h, 3, e, 1 - e)
+            store_out(h, 3)
+        for h in range(2):
+            cast_out(h, 3, h)
+            q_out(h, 3)
+            store_scales(h)

@@ -15,8 +15,6 @@ ACT = mybir.ActivationFunctionType
 ALU = mybir.AluOpType
 
 P = 128
-NV1 = 4
-NV2 = 8
 
 
 def tile_compacterhypercomplexadapter_x1_kernel(
@@ -29,18 +27,25 @@ def tile_compacterhypercomplexadapter_x1_kernel(
         psum = ctx.enter_context(tc.psum_pool(name="psum", bufs=8))
         ctx.enter_context(tc.manual_schedule())
 
-        v1_raw = keep.tile([P, 4, 2, 128], BF16, name="v1_raw", align_bytes=64)
-        nc.sync.dma_start(out=v1_raw[:], in_=v1.rearrange("i (j h) q -> j i h q", h=2))
-        v2_raw = keep.tile([P, 4, 256], BF16, name="v2_raw", align_bytes=64)
-        nc.sync.dma_start(out=v2_raw[:], in_=v2.rearrange("i q m -> q i m"))
-        a_bf = keep.tile([P, 64], BF16, name="a_bf", align_bytes=64)
-        nc.scalar.dma_start(out=a_bf[:], in_=a.rearrange("i r c -> (i r c)").partition_broadcast(P))
+        warm = keep.tile([P, 2], F32, name="warm", align_bytes=64)
+        nc.vector.memset(warm[:], 0.0)
         gd = keep.tile([P, 2, 4], BF16, name="gd", align_bytes=64)
         nc.scalar.dma_start(out=gd[:], in_=g_down.rearrange("(g p t) -> p g t", g=2, t=4))
+        a_bf = keep.tile([P, 4, 4, 4], BF16, name="a_bf", align_bytes=64)
+        nc.scalar.dma_start(
+            out=a_bf[:].rearrange("p i r c -> p (i r c)"), in_=a.rearrange("i r c -> (i r c)").partition_broadcast(P)
+        )
+        v1_raw = keep.tile([P, 4, 2, 128], BF16, name="v1_raw", align_bytes=64)
+        nc.sync.dma_start(out=v1_raw[:], in_=v1.rearrange("i (j h) q -> j i h q", h=2))
+        v1d = keep.tile([P, 4, 4, 128], BF16, name="v1d", align_bytes=64)
+        for r in range(2):
+            nc.sync.dma_start(out=v1d[64 * r : 64 * r + 64], in_=v1.rearrange("i (p t) q -> p i t q", t=4))
         gu = keep.tile([P, 4], BF16, name="gu", align_bytes=64)
         nc.scalar.dma_start(out=gu[:], in_=g_up.rearrange("(p t) -> p t", t=4))
         gm = keep.tile([P, 4], BF16, name="gm", align_bytes=64)
         nc.scalar.dma_start(out=gm[:], in_=g_mid.rearrange("(p t) -> p t", t=4))
+        v2_raw = keep.tile([P, 4, 256], BF16, name="v2_raw", align_bytes=64)
+        nc.sync.dma_start(out=v2_raw[:], in_=v2.rearrange("i q m -> q i m"))
         x_raw = {}
         for h in range(2):
             xv = x[512 * h : 512 * h + 512, :].rearrange("(p t) k -> p t k", t=4)
@@ -53,74 +58,116 @@ def tile_compacterhypercomplexadapter_x1_kernel(
         make_identity(nc, id32[:])
         id16 = keep.tile([P, 128], BF16, name="id16", align_bytes=64)
         make_identity(nc, id16[:])
-
-        warm = keep.tile([P, 2], F32, name="warm", align_bytes=64)
-        nc.vector.memset(warm[:], 0.0)
         nc.scalar.activation(out=warm[:, 0:1], in_=warm[:, 1:2], func=ACT.Gelu)
-        a32 = keep.tile([P, 64], F32, name="a32", align_bytes=64)
-        nc.vector.tensor_copy(out=a32[:], in_=a_bf[:])
+        a1 = keep.tile([P, 2, 4, 4], F32, name="a1", align_bytes=64)
+        for r in range(2):
+            rows = slice(64 * r, 64 * r + 64)
+            nc.gpsimd.tensor_copy(
+                out=a1[rows], in_=a_bf[rows].rearrange("p i (g s) c -> p g s i c", s=2)[:, :, r, :, :]
+            )
+        a32 = keep.tile([P, 4, 4, 4], F32, name="a32", align_bytes=64)
+        nc.gpsimd.tensor_copy(out=a32[:], in_=a_bf[:])
 
         def bank(name, dtype=F32, shape=(P, 512)):
             return psum.tile(list(shape), dtype, name=name, tag="bank")
 
-        def product(engine, out, in_, i, r, c):
-            s = i * 16 + r * 4 + c
-            if engine == 0:
-                nc.vector.tensor_scalar(out=out, in0=in_, scalar1=a32[:, s : s + 1], scalar2=None, op0=ALU.mult)
-            else:
-                nc.scalar.activation(out=out, in_=in_, func=ACT.Copy, scale=a32[:, s : s + 1])
-
-        v1T = keep.tile([P, 4, 2, 128], BF16, name="v1T", align_bytes=64)
-        v2T = keep.tile([P, 4, 2, 128], BF16, name="v2T", align_bytes=64)
-
-        def turn_v1():
-            for k in range(2):
-                b = bank("vb", BF16, (P, 2, 2, 128))
-                for i in range(2):
-                    for h in range(2):
-                        nc.tensor.transpose(b[:, i, h, :], v1_raw[:, 2 * k + i, h, :], id16[:])
-                if k == 0:
-                    nc.scalar.copy(out=v1T[:, 0:2], in_=b[:])
-                else:
-                    nc.vector.tensor_copy(out=v1T[:, 2:4], in_=b[:])
-
-        def turn_v2():
-            for k in range(2):
-                b = bank("vb", BF16, (P, 2, 2, 128))
-                for i in range(2):
-                    for h in range(2):
-                        nc.tensor.transpose(b[:, i, h, :], v2_raw[:, 2 * k + i, 128 * h : 128 * h + 128], id16[:])
-                if k == 0:
-                    nc.scalar.copy(out=v2T[:, 0:2], in_=b[:])
-                else:
-                    nc.vector.tensor_copy(out=v2T[:, 2:4], in_=b[:])
-
-        prods = {}
         banks = {}
 
-        def prod1(u, nv):
-            g, c = divmod(u, 4)
-            pt = work.tile([P, 4, 4, 2, 64], F32, name="p1", bufs=3, align_bytes=64)
-            prods[1, u] = pt
-            for n in range(8):
-                i, rr = divmod(n, 2)
-                product(
-                    0 if n < nv else 1,
-                    pt[:, i, :, rr, :].rearrange("p (b h) w -> p b h w", h=2),
+        def scaled(engine, out, in_, scale):
+            if engine == 0:
+                nc.vector.tensor_scalar(out=out, in0=in_, scalar1=scale, scalar2=None, op0=ALU.mult)
+            elif engine == 1:
+                nc.scalar.activation(out=out, in_=in_, func=ACT.Copy, scale=scale)
+            else:
+                nc.gpsimd.tensor_scalar(out=out, in0=in_, scalar1=scale, scalar2=1.0, op0=ALU.mult, op1=ALU.mult)
+
+        v1p = {}
+        for i in range(1, 4):
+            v1p[i] = keep.tile([P, 512], BF16, name="v1p%d" % i, align_bytes=64)
+
+        def permute1(i, engine):
+            out = v1p[i][:].rearrange("p (t s w) -> p t s w", t=4, s=4)
+            in_ = v1d[:, i].rearrange("p t (w s) -> p t s w", s=4)
+            if engine == 0:
+                nc.vector.tensor_copy(out=out, in_=in_)
+            elif engine == 1:
+                nc.scalar.copy(out=out, in_=in_)
+            else:
+                nc.gpsimd.tensor_scalar(out=out, in0=in_, scalar1=1.0, scalar2=1.0, op0=ALU.mult, op1=ALU.mult)
+
+        acc1 = {}
+
+        def first1(g, c, engine):
+            acc1[g, c] = keep.tile([P, 512], F32, name="acc1_%d%d" % (g, c), align_bytes=64)
+            scaled(
+                engine,
+                acc1[g, c][:].rearrange("p (t s w) -> p t s w", t=4, s=4),
+                v1d[:, 0].rearrange("p t (w s) -> p t s w", s=4),
+                a1[:, g, 0, c : c + 1],
+            )
+
+        def next1(g, c, i):
+            nc.vector.scalar_tensor_tensor(
+                out=acc1[g, c][:], in0=v1p[i][:], scalar=a1[:, g, i, c : c + 1], in1=acc1[g, c][:],
+                op0=ALU.mult, op1=ALU.add,
+            )
+
+        v1T = keep.tile([P, 4, 2, 128], BF16, name="v1T", align_bytes=64)
+        prods = {}
+
+        def turn_v1(k):
+            b = bank("vb", BF16, (P, 2, 2, 128))
+            banks["v1", k] = b
+            for i in range(2):
+                for h in range(2):
+                    nc.tensor.transpose(b[:, i, h, :], v1_raw[:, 2 * k + i, h, :], id16[:])
+
+        def v1_out(k, engine):
+            (nc.vector.tensor_copy if engine == 0 else nc.scalar.copy)(
+                out=v1T[:, 2 * k : 2 * k + 2], in_=banks["v1", k][:]
+            )
+
+        def prod1(g, c, i, engine):
+            if (1, g, c) not in prods:
+                prods[1, g, c] = work.tile(
+                    [P, 4, 4, 2, 64], F32, name="p1", tag="eight", bufs=2, align_bytes=64
+                )
+            for rr in range(2):
+                scaled(
+                    engine,
+                    prods[1, g, c][:, i, :, rr, :].rearrange("p (b h) w -> p b h w", h=2),
                     v1T[:, i].rearrange("p h (w b) -> p b h w", b=2),
-                    i, 2 * g + rr, c,
+                    a32[:, i, 2 * g + rr, c : c + 1],
                 )
 
-        def tr1(u):
-            pt = prods[1, u]
+        def sum_up(out, terms):
+            for i in range(4):
+                nc.tensor.matmul(
+                    out=out, lhsT=terms[i], rhs=id32[:], start=(i == 0), stop=(i == 3), is_transpose=True
+                )
+
+        def tr1(g, c):
             b = bank("u1", F32, (P, 4, 128))
-            banks[1, u] = b
+            banks[1, g, c] = b
             for t in range(4):
-                for i in range(4):
-                    nc.tensor.matmul(
-                        out=b[:, t, :], lhsT=pt[:, i, t].rearrange("p r w -> p (r w)"), rhs=id32[:],
-                        start=(i == 0), stop=(i == 3), is_transpose=True,
-                    )
+                sum_up(b[:, t, :], [prods[1, g, c][:, i, t].rearrange("p r w -> p (r w)") for i in range(4)])
+
+        def fin1(g, c):
+            if (1, g, c) in banks:
+                nc.vector.tensor_tensor(
+                    out=wd_bf[g][:, :, c, :, :],
+                    in0=banks[1, g, c][:].rearrange("p t (w s) -> p s w t", s=4),
+                    in1=gd[:, g, :].unsqueeze(1).unsqueeze(1).to_broadcast([P, 4, 32, 4]),
+                    op=ALU.mult,
+                )
+                return
+            for s in range(4):
+                nc.vector.tensor_tensor(
+                    out=wd_bf[g][:, s, c].rearrange("p (b w) t -> p b t w", w=4),
+                    in0=acc1[g, c][:].rearrange("p (t s b w) -> p s b t w", t=4, s=4, w=4)[:, s],
+                    in1=gd[:, g, :].unsqueeze(1).unsqueeze(3).to_broadcast([P, 8, 4, 4]),
+                    op=ALU.mult,
+                )
 
         wd_bf = {}
         wd_codes = {}
@@ -130,45 +177,40 @@ def tile_compacterhypercomplexadapter_x1_kernel(
             wd_codes[g] = keep.tile([P, 512], U32, name="wd_codes%d" % g, align_bytes=64)
             wd_scales[g] = keep.tile([P, 512], U8, name="wd_scales%d" % g, align_bytes=64)
 
-        def ev1(u):
-            g, c = divmod(u, 4)
-            nc.vector.tensor_tensor(
-                out=wd_bf[g][:, :, c, :, :],
-                in0=banks[1, u][:].rearrange("p t (w s) -> p s w t", s=4),
-                in1=gd[:, g, :].unsqueeze(1).unsqueeze(1).to_broadcast([P, 4, 32, 4]),
-                op=ALU.mult,
-            )
-
         def q_wd(g):
             nc.vector.quantize_mx(
                 out=wd_codes[g][:].bitcast(FP8), scales=wd_scales[g][:],
                 in_=wd_bf[g][:].rearrange("p s c w t -> p (s c w t)"),
             )
 
-        def prod2_tile(c):
-            prods[2, c] = work.tile([P, 2, 4, 4, 4, 32], F32, name="p2", bufs=3, align_bytes=64)
+        v2T = keep.tile([P, 4, 2, 4, 32], BF16, name="v2T", align_bytes=64)
 
-        def prod2(c, engine, n0, n1):
-            pt = prods[2, c]
-            for n in range(n0, n1):
-                i, r = divmod(n, 4)
-                product(
-                    engine,
-                    pt[:, :, i, :, r, :],
-                    v2T[:, i].rearrange("p h (w t) -> p h t w", t=4),
-                    i, r, c,
-                )
+        def turn_v2(k):
+            b = bank("vb", BF16, (P, 4, 128))
+            banks["v2", k] = b
+            for i in range(2):
+                for h in range(2):
+                    nc.tensor.transpose(
+                        b[:, 2 * i + h, :], v2_raw[:, 2 * k + i, 128 * h : 128 * h + 128], id16[:]
+                    )
+
+        def v2_out(k, engine):
+            (nc.vector.tensor_copy if engine == 0 else nc.scalar.copy)(
+                out=v2T[:, 2 * k : 2 * k + 2].rearrange("p i h t w -> p (i h) t w"),
+                in_=banks["v2", k][:].rearrange("p e (w t) -> p e t w", t=4),
+            )
+
+        def prod2(c, i, engine):
+            if (2, c) not in prods:
+                prods[2, c] = work.tile([P, 2, 4, 4, 4, 32], F32, name="p2", bufs=4, align_bytes=64)
+            for r in range(4):
+                scaled(engine, prods[2, c][:, :, i, :, r, :], v2T[:, i], a32[:, i, r, c : c + 1])
 
         def tr2(c, h):
-            pt = prods[2, c]
             b = bank("u2", F32, (P, 4, 128))
             banks[2, c, h] = b
             for t in range(4):
-                for i in range(4):
-                    nc.tensor.matmul(
-                        out=b[:, t, :], lhsT=pt[:, h, i, t].rearrange("p r w -> p (r w)"), rhs=id32[:],
-                        start=(i == 0), stop=(i == 3), is_transpose=True,
-                    )
+                sum_up(b[:, t, :], [prods[2, c][:, h, i, t].rearrange("p r w -> p (r w)") for i in range(4)])
 
         wu_bf = {}
         wu_codes = {}
@@ -229,7 +271,6 @@ def tile_compacterhypercomplexadapter_x1_kernel(
         u_codes = {}
         u_scales = {}
         for h in range(2):
-            hg[h] = keep.tile([P, 4, 512], F32, name="hg%d" % h, align_bytes=64)
             u_codes[h] = keep.tile([P, 512], U32, name="u_codes%d" % h, align_bytes=64)
             u_scales[h] = keep.tile([P, 512], U8, name="u_scales%d" % h, align_bytes=64)
             for k in range(2):
@@ -245,13 +286,18 @@ def tile_compacterhypercomplexadapter_x1_kernel(
                     rhs=x_codes[h, g][:].bitcast(FP8), rhs_scale=x_scales[h, g][:],
                     start=(g == 0), stop=(g == 1),
                 )
-            nc.scalar.activation(out=hg[h][:, s, :], in_=b[:], func=ACT.Gelu)
+            banks["h", h, s] = b
+
+        def gelu(h, s):
+            if h not in hg:
+                hg[h] = work.tile([P, 4, 512], F32, name="hg", tag="eight", bufs=2, align_bytes=64)
+            nc.scalar.activation(out=hg[h][:, s, :], in_=banks["h", h, s][:], func=ACT.Gelu)
 
         def u_mul(h, k):
             nc.vector.tensor_tensor(
-                out=u_bf[h, k][:],
-                in0=hg[h][:, :, 256 * k : 256 * k + 256].rearrange("p s n -> p n s"),
-                in1=gm[:].unsqueeze(1).to_broadcast([P, 256, 4]),
+                out=u_bf[h, k][:].rearrange("p (b n) s -> p b s n", n=4),
+                in0=hg[h][:, :, 256 * k : 256 * k + 256].rearrange("p s (b n) -> p b s n", n=4),
+                in1=gm[:].unsqueeze(1).unsqueeze(3).to_broadcast([P, 64, 4, 4]),
                 op=ALU.mult,
             )
 
@@ -279,8 +325,8 @@ def tile_compacterhypercomplexadapter_x1_kernel(
                 )
 
         def out_copy(h, c, e, engine):
-            if e == 0:
-                of[h, c] = work.tile([P, 4, 256], F32, name="of", bufs=4, align_bytes=64)
+            if (h, c) not in of:
+                of[h, c] = keep.tile([P, 4, 256], F32, name="of%d%d" % (h, c), align_bytes=64)
             (nc.vector.tensor_copy if engine == 0 else nc.scalar.copy)(
                 out=of[h, c][:, 2 * e : 2 * e + 2, :], in_=banks[3, h, c, e][:]
             )
@@ -294,7 +340,8 @@ def tile_compacterhypercomplexadapter_x1_kernel(
         def cast_out(h, c, engine):
             ob[h, c] = work.tile([P, 256, 4], BF16, name="ob_bf", bufs=4, align_bytes=64)
             (nc.vector.tensor_copy if engine == 0 else nc.scalar.copy)(
-                out=ob[h, c][:], in_=of[h, c][:].rearrange("p t n -> p n t")
+                out=ob[h, c][:].rearrange("p (b n) t -> p b t n", n=4),
+                in_=of[h, c][:].rearrange("p t (b n) -> p b t n", n=4),
             )
 
         oc = {}
@@ -319,118 +366,196 @@ def tile_compacterhypercomplexadapter_x1_kernel(
                     in_=osc[h][32 * qd : 32 * qd + 4, :].bitcast(I32),
                 )
 
-        turn_v1()
-        turn_v2()
-        prod1(0, 4)
-        prod1(1, 4)
-        for u in range(8):
-            tr1(u)
-            if u in (2, 3, 4, 5):
-                x_turn(u - 2)
-            if u + 2 < 8:
-                prod1(u + 2, 4)
-            if u == 6:
-                prod2_tile(0)
-                prod2(0, 0, 0, 6)
-                prod2(0, 1, 6, 11)
-            if u == 7:
-                prod2(0, 1, 11, 16)
-            ev1(u)
-            if u in (2, 3, 4, 5):
-                x_out(u - 2, 1)
-            if u == 3:
-                q_wd(0)
-            if u == 4:
-                q_x(0, 0)
-            if u == 5:
-                q_x(0, 1)
-        prod2_tile(1)
-        tr2(0, 0)
-        q_wd(1)
-        prod2(1, 0, 0, 6)
-        prod2(1, 1, 6, 11)
-        tr2(0, 1)
-        ev2(0, 0)
-        for s in range(4):
-            mm1(0, s)
-        ev2(0, 1)
-        x_turn(4)
-        x_turn(5)
-        x_out(4, 0)
-        x_out(5, 0)
-        prod2(1, 1, 11, 16)
-        q_wu(0)
-        tr2(1, 0)
-        u_mul(0, 0)
-        u_mul(0, 1)
-        q_u(0, 0)
-        q_u(0, 1)
-        x_turn(6)
+        turn_v1(0)
+        turn_v1(1)
+        first1(0, 2, 0)
+        first1(0, 0, 1)
+        permute1(1, 2)
+        first1(1, 1, 0)
+        turn_v2(0)
+        v1_out(0, 1)
+        v1_out(1, 0)
+        permute1(2, 2)
+        first1(0, 1, 1)
+        next1(0, 2, 1)
+        turn_v2(1)
+        v2_out(0, 1)
+        next1(0, 1, 1)
+        x_turn(1)
+        prod2(2, 0, 1)
+        prod1(1, 3, 2, 0)
+        next1(0, 0, 1)
+        x_turn(2)
+        next1(1, 1, 1)
+        prod2(0, 1, 1)
+        x_turn(0)
+        prod1(1, 3, 1, 0)
+        x_turn(3)
+        next1(0, 1, 2)
+        prod2(3, 0, 1)
+        prod1(0, 3, 2, 0)
         x_turn(7)
-        x_out(6, 1)
-        x_out(7, 1)
-        ev2(1, 0)
-        prod2_tile(2)
-        prod2(2, 0, 0, 6)
-        q_x(1, 0)
-        q_x(1, 1)
-        prod2(2, 1, 6, 16)
-        tr2(1, 1)
-        ev2(1, 1)
-        for e in range(2):
-            mm2(0, 0, e)
-            out_copy(0, 0, e, 1)
-        store_out(0, 0)
-        q_wu(1)
-        for s in range(4):
-            mm1(1, s)
-        cast_out(0, 0, 0)
+        prod1(0, 3, 0, 0)
+        prod1(0, 3, 1, 0)
+        prod1(1, 3, 0, 0)
+        x_out(1, 1)
+        x_turn(5)
+        v2_out(1, 0)
+        first1(1, 0, 1)
+        prod2(2, 2, 0)
+        x_turn(4)
+        x_out(0, 1)
+        next1(1, 0, 1)
+        x_turn(6)
+        prod2(2, 1, 1)
+        prod2(2, 3, 0)
+        next1(1, 0, 2)
+        x_out(2, 1)
         tr2(2, 0)
-        q_out(0, 0)
-        prod2_tile(3)
-        prod2(3, 0, 0, 6)
-        u_mul(1, 0)
-        u_mul(1, 1)
-        for e in range(2):
-            mm2(0, 1, e)
-            out_copy(0, 1, e, 1)
-        store_out(0, 1)
-        q_u(1, 0)
-        q_u(1, 1)
-        tr2(2, 1)
-        prod2(3, 1, 6, 16)
+        next1(1, 1, 2)
+        prod2(0, 2, 1)
+        q_x(0, 0)
+        next1(0, 2, 2)
+        prod1(1, 3, 3, 1)
+        prod2(0, 3, 0)
+        prod1(0, 3, 3, 1)
+        next1(0, 0, 2)
+        tr1(1, 3)
+        permute1(3, 1)
         ev2(2, 0)
-        cast_out(0, 1, 0)
+        x_out(3, 1)
+        next1(0, 1, 3)
+        prod2(1, 1, 1)
+        q_x(0, 1)
+        fin1(0, 1)
+        prod2(3, 2, 1)
+        tr2(2, 1)
+        next1(0, 0, 3)
+        fin1(1, 3)
+        x_out(7, 1)
+        next1(0, 2, 3)
+        prod2(1, 3, 1)
+        next1(1, 1, 3)
+        next1(1, 0, 3)
+        tr1(0, 3)
+        prod2(0, 0, 1)
+        fin1(1, 0)
+        fin1(0, 2)
+        prod2(3, 3, 1)
+        fin1(0, 0)
+        fin1(1, 1)
+        tr2(0, 1)
+        first1(1, 2, 1)
+        fin1(0, 3)
+        x_out(5, 1)
+        next1(1, 2, 1)
+        x_out(6, 1)
+        prod2(1, 2, 1)
+        next1(1, 2, 2)
+        q_wd(0)
+        tr2(0, 0)
+        prod2(3, 1, 1)
+        next1(1, 2, 3)
+        fin1(1, 2)
+        x_out(4, 1)
+        q_wd(1)
+        prod2(1, 0, 1)
+        q_x(1, 0)
+        mm1(0, 0)
+        ev2(0, 0)
+        ev2(0, 1)
+        mm1(0, 2)
+        gelu(0, 0)
+        q_wu(0)
+        mm1(0, 3)
+        gelu(0, 2)
+        q_x(1, 1)
+        mm1(0, 1)
+        gelu(0, 3)
         ev2(2, 1)
-        q_out(0, 1)
-        for c in range(2):
-            for e in range(2):
-                mm2(1, c, e)
-                out_copy(1, c, e, 1)
-            store_out(1, c)
+        gelu(0, 1)
+        mm1(1, 1)
         q_wu(2)
-        tr2(3, 0)
-        cast_out(1, 0, 0)
-        q_out(1, 0)
+        u_mul(0, 0)
+        mm1(1, 2)
+        gelu(1, 1)
+        mm1(1, 3)
+        gelu(1, 2)
+        mm1(1, 0)
+        q_u(0, 0)
+        gelu(1, 3)
+        u_mul(0, 1)
+        mm2(0, 2, 0)
+        gelu(1, 0)
+        mm2(0, 0, 0)
+        tr2(1, 0)
+        out_copy(0, 2, 0, 1)
+        q_u(0, 1)
+        out_copy(0, 0, 0, 1)
+        u_mul(1, 1)
+        mm2(0, 0, 1)
+        mm2(0, 2, 1)
+        ev2(1, 0)
+        out_copy(0, 0, 1, 1)
         tr2(3, 1)
-        cast_out(1, 1, 0)
-        ev2(3, 0)
+        out_copy(0, 2, 1, 0)
+        cast_out(0, 0, 1)
+        store_out(0, 0)
+        q_u(1, 1)
+        u_mul(1, 0)
+        mm2(1, 0, 1)
+        cast_out(0, 2, 1)
+        store_out(0, 2)
+        mm2(1, 2, 1)
+        tr2(3, 0)
+        q_out(0, 0)
+        q_u(1, 0)
+        out_copy(1, 0, 1, 1)
+        q_out(0, 2)
         ev2(3, 1)
-        q_out(1, 1)
+        out_copy(1, 2, 1, 1)
+        mm2(1, 0, 0)
+        ev2(3, 0)
+        mm2(1, 2, 0)
+        out_copy(1, 0, 0, 1)
+        tr2(1, 1)
         q_wu(3)
+        out_copy(1, 2, 0, 1)
+        store_out(1, 0)
+        cast_out(1, 0, 0)
+        cast_out(1, 2, 1)
+        q_out(1, 0)
+        mm2(1, 3, 0)
+        store_out(1, 2)
+        ev2(1, 1)
+        mm2(1, 3, 1)
+        mm2(0, 3, 0)
+        out_copy(1, 3, 1, 1)
+        q_out(1, 2)
+        mm2(0, 3, 1)
+        out_copy(1, 3, 0, 0)
+        out_copy(0, 3, 1, 1)
+        q_wu(1)
+        out_copy(0, 3, 0, 1)
+        store_out(1, 3)
+        cast_out(1, 3, 0)
+        mm2(1, 1, 0)
+        mm2(0, 1, 0)
+        cast_out(0, 3, 1)
+        mm2(1, 1, 1)
+        q_out(1, 3)
+        mm2(0, 1, 1)
+        store_out(0, 3)
+        out_copy(0, 1, 0, 0)
+        out_copy(1, 1, 1, 1)
+        q_out(0, 3)
+        out_copy(0, 1, 1, 0)
+        out_copy(1, 1, 0, 0)
+        cast_out(0, 1, 1)
+        store_out(0, 1)
+        cast_out(1, 1, 0)
+        store_out(1, 1)
+        q_out(1, 1)
+        q_out(0, 1)
         for h in range(2):
-            for e in range(2):
-                mm2(h, 2, e)
-                out_copy(h, 2, e, 1)
-            store_out(h, 2)
-            cast_out(h, 2, 0)
-            q_out(h, 2)
-        for h in range(2):
-            for e in range(2):
-                mm2(h, 3, e)
-                out_copy(h, 3, e, 1 - e)
-            store_out(h, 3)
-        for h in range(2):
-            cast_out(h, 3, h)
-            q_out(h, 3)
             store_scales(h)

from contextlib import ExitStack

import concourse.mybir as mybir
from concourse.masks import make_identity

FLOPS = 2 * 1024 * 1024 * 512 * 2

F32 = mybir.dt.float32
BF16 = mybir.dt.bfloat16
U32 = mybir.dt.uint32
I32 = mybir.dt.int32
U8 = mybir.dt.uint8
FP8 = mybir.dt.float8_e4m3fn_x4
ACT = mybir.ActivationFunctionType
ALU = mybir.AluOpType

P = 128


def tile_compacterhypercomplexadapter_x1_kernel(
    tc, x, a, v1, v2, g_down, g_mid, g_up, out_0, out_1, out_2
):
    nc = tc.nc
    with ExitStack() as ctx:
        keep = ctx.enter_context(tc.tile_pool(name="keep", bufs=1))
        work = ctx.enter_context(tc.tile_pool(name="work", bufs=2))
        psum = ctx.enter_context(tc.psum_pool(name="psum", bufs=8))
        ctx.enter_context(tc.manual_schedule())

        warm = keep.tile([P, 2], F32, name="warm", align_bytes=64)
        nc.vector.memset(warm[:], 0.0)
        gd = keep.tile([P, 2, 4], BF16, name="gd", align_bytes=64)
        nc.scalar.dma_start(out=gd[:], in_=g_down.rearrange("(g p t) -> p g t", g=2, t=4))
        a_bf = keep.tile([P, 4, 4, 4], BF16, name="a_bf", align_bytes=64)
        nc.scalar.dma_start(
            out=a_bf[:].rearrange("p i r c -> p (i r c)"), in_=a.rearrange("i r c -> (i r c)").partition_broadcast(P)
        )
        v1_raw = keep.tile([P, 4, 2, 128], BF16, name="v1_raw", align_bytes=64)
        nc.sync.dma_start(out=v1_raw[:], in_=v1.rearrange("i (j h) q -> j i h q", h=2))
        v1d = keep.tile([P, 4, 4, 128], BF16, name="v1d", align_bytes=64)
        for r in range(2):
            nc.sync.dma_start(out=v1d[64 * r : 64 * r + 64], in_=v1.rearrange("i (p t) q -> p i t q", t=4))
        gu = keep.tile([P, 4], BF16, name="gu", align_bytes=64)
        nc.scalar.dma_start(out=gu[:], in_=g_up.rearrange("(p t) -> p t", t=4))
        gm = keep.tile([P, 4], BF16, name="gm", align_bytes=64)
        nc.scalar.dma_start(out=gm[:], in_=g_mid.rearrange("(p t) -> p t", t=4))
        v2_raw = keep.tile([P, 4, 256], BF16, name="v2_raw", align_bytes=64)
        nc.sync.dma_start(out=v2_raw[:], in_=v2.rearrange("i q m -> q i m"))
        x_raw = {}
        for h in range(2):
            xv = x[512 * h : 512 * h + 512, :].rearrange("(p t) k -> p t k", t=4)
            for tp in range(2):
                xt = keep.tile([P, 2, 1024], BF16, name="x_raw_%d%d" % (h, tp), align_bytes=64)
                nc.sync.dma_start(out=xt[:], in_=xv[:, 2 * tp : 2 * tp + 2, :])
                x_raw[h, tp] = xt

        id32 = keep.tile([P, 128], F32, name="id32", align_bytes=64)
        make_identity(nc, id32[:])
        id16 = keep.tile([P, 128], BF16, name="id16", align_bytes=64)
        make_identity(nc, id16[:])
        nc.scalar.activation(out=warm[:, 0:1], in_=warm[:, 1:2], func=ACT.Gelu)
        a1 = keep.tile([P, 2, 4, 4], F32, name="a1", align_bytes=64)
        for r in range(2):
            rows = slice(64 * r, 64 * r + 64)
            nc.gpsimd.tensor_copy(
                out=a1[rows], in_=a_bf[rows].rearrange("p i (g s) c -> p g s i c", s=2)[:, :, r, :, :]
            )
        a32 = keep.tile([P, 4, 4, 4], F32, name="a32", align_bytes=64)
        nc.gpsimd.tensor_copy(out=a32[:], in_=a_bf[:])

        def bank(name, dtype=F32, shape=(P, 512)):
            return psum.tile(list(shape), dtype, name=name, tag="bank")

        banks = {}

        def scaled(engine, out, in_, scale):
            if engine == 0:
                nc.vector.tensor_scalar(out=out, in0=in_, scalar1=scale, scalar2=None, op0=ALU.mult)
            elif engine == 1:
                nc.scalar.activation(out=out, in_=in_, func=ACT.Copy, scale=scale)
            else:
                nc.gpsimd.tensor_scalar(out=out, in0=in_, scalar1=scale, scalar2=1.0, op0=ALU.mult, op1=ALU.mult)

        v1p = {}
        for i in range(1, 4):
            v1p[i] = keep.tile([P, 512], BF16, name="v1p%d" % i, align_bytes=64)

        def permute1(i, engine):
            out = v1p[i][:].rearrange("p (t s w) -> p t s w", t=4, s=4)
            in_ = v1d[:, i].rearrange("p t (w s) -> p t s w", s=4)
            if engine == 0:
                nc.vector.tensor_copy(out=out, in_=in_)
            elif engine == 1:
                nc.scalar.copy(out=out, in_=in_)
            else:
                nc.gpsimd.tensor_scalar(out=out, in0=in_, scalar1=1.0, scalar2=1.0, op0=ALU.mult, op1=ALU.mult)

        acc1 = {}

        def first1(g, c, engine):
            acc1[g, c] = keep.tile([P, 512], F32, name="acc1_%d%d" % (g, c), align_bytes=64)
            scaled(
                engine,
                acc1[g, c][:].rearrange("p (t s w) -> p t s w", t=4, s=4),
                v1d[:, 0].rearrange("p t (w s) -> p t s w", s=4),
                a1[:, g, 0, c : c + 1],
            )

        def next1(g, c, i):
            nc.vector.scalar_tensor_tensor(
                out=acc1[g, c][:], in0=v1p[i][:], scalar=a1[:, g, i, c : c + 1], in1=acc1[g, c][:],
                op0=ALU.mult, op1=ALU.add,
            )

        v1T = keep.tile([P, 4, 2, 128], BF16, name="v1T", align_bytes=64)
        prods = {}

        def turn_v1(k):
            b = bank("vb", BF16, (P, 2, 2, 128))
            banks["v1", k] = b
            for i in range(2):
                for h in range(2):
                    nc.tensor.transpose(b[:, i, h, :], v1_raw[:, 2 * k + i, h, :], id16[:])

        def v1_out(k, engine):
            (nc.vector.tensor_copy if engine == 0 else nc.scalar.copy)(
                out=v1T[:, 2 * k : 2 * k + 2], in_=banks["v1", k][:]
            )

        def prod1(g, c, i, engine):
            if (1, g, c) not in prods:
                prods[1, g, c] = work.tile(
                    [P, 4, 4, 2, 64], F32, name="p1", tag="eight", bufs=2, align_bytes=64
                )
            for rr in range(2):
                scaled(
                    engine,
                    prods[1, g, c][:, i, :, rr, :].rearrange("p (b h) w -> p b h w", h=2),
                    v1T[:, i].rearrange("p h (w b) -> p b h w", b=2),
                    a32[:, i, 2 * g + rr, c : c + 1],
                )

        def sum_up(out, terms):
            for i in range(4):
                nc.tensor.matmul(
                    out=out, lhsT=terms[i], rhs=id32[:], start=(i == 0), stop=(i == 3), is_transpose=True
                )

        def tr1(g, c):
            b = bank("u1", F32, (P, 4, 128))
            banks[1, g, c] = b
            for t in range(4):
                sum_up(b[:, t, :], [prods[1, g, c][:, i, t].rearrange("p r w -> p (r w)") for i in range(4)])

        def fin1(g, c):
            if (1, g, c) in banks:
                nc.vector.tensor_tensor(
                    out=wd_bf[g][:, :, c, :, :],
                    in0=banks[1, g, c][:].rearrange("p t (w s) -> p s w t", s=4),
                    in1=gd[:, g, :].unsqueeze(1).unsqueeze(1).to_broadcast([P, 4, 32, 4]),
                    op=ALU.mult,
                )
                return
            for s in range(4):
                nc.vector.tensor_tensor(
                    out=wd_bf[g][:, s, c].rearrange("p (b w) t -> p b t w", w=4),
                    in0=acc1[g, c][:].rearrange("p (t s b w) -> p s b t w", t=4, s=4, w=4)[:, s],
                    in1=gd[:, g, :].unsqueeze(1).unsqueeze(3).to_broadcast([P, 8, 4, 4]),
                    op=ALU.mult,
                )

        wd_bf = {}
        wd_codes = {}
        wd_scales = {}
        for g in range(2):
            wd_bf[g] = keep.tile([P, 4, 4, 32, 4], BF16, name="wd_bf%d" % g, align_bytes=64)
            wd_codes[g] = keep.tile([P, 512], U32, name="wd_codes%d" % g, align_bytes=64)
            wd_scales[g] = keep.tile([P, 512], U8, name="wd_scales%d" % g, align_bytes=64)

        def q_wd(g):
            nc.vector.quantize_mx(
                out=wd_codes[g][:].bitcast(FP8), scales=wd_scales[g][:],
                in_=wd_bf[g][:].rearrange("p s c w t -> p (s c w t)"),
            )

        v2T = keep.tile([P, 4, 2, 4, 32], BF16, name="v2T", align_bytes=64)

        def turn_v2(k):
            b = bank("vb", BF16, (P, 4, 128))
            banks["v2", k] = b
            for i in range(2):
                for h in range(2):
                    nc.tensor.transpose(
                        b[:, 2 * i + h, :], v2_raw[:, 2 * k + i, 128 * h : 128 * h + 128], id16[:]
                    )

        def v2_out(k, engine):
            (nc.vector.tensor_copy if engine == 0 else nc.scalar.copy)(
                out=v2T[:, 2 * k : 2 * k + 2].rearrange("p i h t w -> p (i h) t w"),
                in_=banks["v2", k][:].rearrange("p e (w t) -> p e t w", t=4),
            )

        def prod2(c, i, engine):
            if (2, c) not in prods:
                prods[2, c] = work.tile([P, 2, 4, 4, 4, 32], F32, name="p2", bufs=4, align_bytes=64)
            for r in range(4):
                scaled(engine, prods[2, c][:, :, i, :, r, :], v2T[:, i], a32[:, i, r, c : c + 1])

        def tr2(c, h):
            b = bank("u2", F32, (P, 4, 128))
            banks[2, c, h] = b
            for t in range(4):
                sum_up(b[:, t, :], [prods[2, c][:, h, i, t].rearrange("p r w -> p (r w)") for i in range(4)])

        wu_bf = {}
        wu_codes = {}
        wu_scales = {}
        for c in range(4):
            wu_codes[c] = keep.tile([P, 256], U32, name="wu_codes%d" % c, align_bytes=64)
            wu_scales[c] = keep.tile([P, 256], U8, name="wu_scales%d" % c, align_bytes=64)
            wu_bf[c] = keep.tile([P, 256, 4], BF16, name="wu_bf%d" % c, align_bytes=64)

        def ev2(c, h):
            nc.vector.tensor_tensor(
                out=wu_bf[c][:, 128 * h : 128 * h + 128, :],
                in0=banks[2, c, h][:].rearrange("p t m -> p m t"),
                in1=gu[:].unsqueeze(1).to_broadcast([P, 128, 4]),
                op=ALU.mult,
            )

        def q_wu(c):
            nc.vector.quantize_mx(
                out=wu_codes[c][:].bitcast(FP8), scales=wu_scales[c][:],
                in_=wu_bf[c][:].rearrange("p m t -> p (m t)"),
            )

        x_bf = {}
        x_codes = {}
        x_scales = {}
        for h in range(2):
            for g in range(2):
                x_bf[h, g] = keep.tile([P, 512, 4], BF16, name="x_bf%d%d" % (h, g), align_bytes=64)
                x_codes[h, g] = keep.tile([P, 512], U32, name="x_codes%d%d" % (h, g), align_bytes=64)
                x_scales[h, g] = keep.tile([P, 512], U8, name="x_scales%d%d" % (h, g), align_bytes=64)

        def x_turn(j):
            h, tp, g = j // 4, (j // 2) % 2, j % 2
            b = bank("xb", F32, (P, 2, 2, 128))
            banks[0, j] = b
            for k in range(2):
                words = x_raw[h, tp][:, k, :].bitcast(F32)
                for u in range(2):
                    nc.tensor.transpose(b[:, k, u, :], words[:, 256 * g + u : 256 * (g + 1) : 2], id32[:])

        def x_out(j, engine):
            h, tp, g = j // 4, (j // 2) % 2, j % 2
            dst = x_bf[h, g][:, 256 * tp : 256 * tp + 256, :].rearrange("p n t -> p (n t)").bitcast(F32)
            (nc.vector.tensor_copy if engine == 0 else nc.scalar.copy)(
                out=dst.rearrange("p (k r u) -> p k r u", k=2, u=2),
                in_=banks[0, j][:].rearrange("p k u r -> p k r u"),
            )

        def q_x(h, g):
            nc.vector.quantize_mx(
                out=x_codes[h, g][:].bitcast(FP8), scales=x_scales[h, g][:],
                in_=x_bf[h, g][:].rearrange("p n t -> p (n t)"),
            )

        hg = {}
        u_bf = {}
        u_codes = {}
        u_scales = {}
        for h in range(2):
            u_codes[h] = keep.tile([P, 512], U32, name="u_codes%d" % h, align_bytes=64)
            u_scales[h] = keep.tile([P, 512], U8, name="u_scales%d" % h, align_bytes=64)
            for k in range(2):
                u_bf[h, k] = keep.tile([P, 256, 4], BF16, name="u_bf%d%d" % (h, k), align_bytes=64)

        def mm1(h, s):
            b = bank("hb")
            for g in range(2):
                nc.tensor.matmul_mx(
                    out=b[:],
                    lhsT=wd_codes[g][:, 128 * s : 128 * s + 128].bitcast(FP8),
                    lhsT_scale=wd_scales[g][:, 128 * s : 128 * s + 128],
                    rhs=x_codes[h, g][:].bitcast(FP8), rhs_scale=x_scales[h, g][:],
                    start=(g == 0), stop=(g == 1),
                )
            banks["h", h, s] = b

        def gelu(h, s):
            if h not in hg:
                hg[h] = work.tile([P, 4, 512], F32, name="hg", tag="eight", bufs=2, align_bytes=64)
            nc.scalar.activation(out=hg[h][:, s, :], in_=banks["h", h, s][:], func=ACT.Gelu)

        def u_mul(h, k):
            nc.vector.tensor_tensor(
                out=u_bf[h, k][:].rearrange("p (b n) s -> p b s n", n=4),
                in0=hg[h][:, :, 256 * k : 256 * k + 256].rearrange("p s (b n) -> p b s n", n=4),
                in1=gm[:].unsqueeze(1).unsqueeze(3).to_broadcast([P, 64, 4, 4]),
                op=ALU.mult,
            )

        def q_u(h, k):
            nc.vector.quantize_mx(
                out=u_codes[h][:, 256 * k : 256 * k + 256].bitcast(FP8),
                scales=u_scales[h][:, 256 * k : 256 * k + 256],
                in_=u_bf[h, k][:].rearrange("p n t -> p (n t)"),
            )

        of = {}
        ob = {}

        def mm2(h, c, e):
            b = bank("ob", F32, (P, 2, 256))
            banks[3, h, c, e] = b
            for k in range(2):
                t = 2 * e + k
                nc.tensor.matmul_mx(
                    out=b[:, k, :],
                    lhsT=u_codes[h][:, 128 * t : 128 * t + 128].bitcast(FP8),
                    lhsT_scale=u_scales[h][:, 128 * t : 128 * t + 128],
                    rhs=wu_codes[c][:].bitcast(FP8), rhs_scale=wu_scales[c][:],
                    start=True, stop=True,
                )

        def out_copy(h, c, e, engine):
            if (h, c) not in of:
                of[h, c] = keep.tile([P, 4, 256], F32, name="of%d%d" % (h, c), align_bytes=64)
            (nc.vector.tensor_copy if engine == 0 else nc.scalar.copy)(
                out=of[h, c][:, 2 * e : 2 * e + 2, :], in_=banks[3, h, c, e][:]
            )

        def store_out(h, c):
            nc.sync.dma_start(
                out=out_0[512 * h : 512 * h + 512, 256 * c : 256 * c + 256].rearrange("(p t) n -> p t n", t=4),
                in_=of[h, c][:],
            )

        def cast_out(h, c, engine):
            ob[h, c] = work.tile([P, 256, 4], BF16, name="ob_bf", bufs=4, align_bytes=64)
            (nc.vector.tensor_copy if engine == 0 else nc.scalar.copy)(
                out=ob[h, c][:].rearrange("p (b n) t -> p b t n", n=4),
                in_=of[h, c][:].rearrange("p t (b n) -> p b t n", n=4),
            )

        oc = {}
        osc = {}
        for h in range(2):
            osc[h] = keep.tile([P, 1024], U8, name="osc%d" % h, align_bytes=64)

        def q_out(h, c):
            cols = slice(256 * c, 256 * c + 256)
            oc[h, c] = work.tile([P, 256], U32, name="oc", bufs=4, align_bytes=64)
            nc.vector.quantize_mx(
                out=oc[h, c][:].bitcast(FP8), scales=osc[h][:, cols], in_=ob[h, c][:].rearrange("p n t -> p (n t)")
            )
            nc.sync.dma_start(
                out=out_1[h, :, cols, :].rearrange("p m t -> p (m t)").bitcast(I32), in_=oc[h, c][:].bitcast(I32)
            )

        def store_scales(h):
            for qd in range(4):
                nc.sync.dma_start(
                    out=out_2[h, 4 * qd : 4 * qd + 4, :].bitcast(I32),
                    in_=osc[h][32 * qd : 32 * qd + 4, :].bitcast(I32),
                )

        turn_v1(0)
        turn_v1(1)
        first1(0, 2, 0)
        first1(0, 0, 1)
        permute1(1, 2)
        first1(1, 1, 0)
        turn_v2(0)
        v1_out(0, 1)
        v1_out(1, 0)
        permute1(2, 2)
        first1(0, 1, 1)
        next1(0, 2, 1)
        turn_v2(1)
        v2_out(0, 1)
        next1(0, 1, 1)
        x_turn(1)
        prod2(2, 0, 1)
        prod1(1, 3, 2, 0)
        next1(0, 0, 1)
        x_turn(2)
        next1(1, 1, 1)
        prod2(0, 1, 1)
        x_turn(0)
        prod1(1, 3, 1, 0)
        x_turn(3)
        next1(0, 1, 2)
        prod2(3, 0, 1)
        prod1(0, 3, 2, 0)
        x_turn(7)
        prod1(0, 3, 0, 0)
        prod1(0, 3, 1, 0)
        prod1(1, 3, 0, 0)
        x_out(1, 1)
        x_turn(5)
        v2_out(1, 0)
        first1(1, 0, 1)
        prod2(2, 2, 0)
        x_turn(4)
        x_out(0, 1)
        next1(1, 0, 1)
        x_turn(6)
        prod2(2, 1, 1)
        prod2(2, 3, 0)
        next1(1, 0, 2)
        x_out(2, 1)
        tr2(2, 0)
        next1(1, 1, 2)
        prod2(0, 2, 1)
        q_x(0, 0)
        next1(0, 2, 2)
        prod1(1, 3, 3, 1)
        prod2(0, 3, 0)
        prod1(0, 3, 3, 1)
        next1(0, 0, 2)
        tr1(1, 3)
        permute1(3, 1)
        ev2(2, 0)
        x_out(3, 1)
        next1(0, 1, 3)
        prod2(1, 1, 1)
        q_x(0, 1)
        fin1(0, 1)
        prod2(3, 2, 1)
        tr2(2, 1)
        next1(0, 0, 3)
        fin1(1, 3)
        x_out(7, 1)
        next1(0, 2, 3)
        prod2(1, 3, 1)
        next1(1, 1, 3)
        next1(1, 0, 3)
        tr1(0, 3)
        prod2(0, 0, 1)
        fin1(1, 0)
        fin1(0, 2)
        prod2(3, 3, 1)
        fin1(0, 0)
        fin1(1, 1)
        tr2(0, 1)
        first1(1, 2, 1)
        fin1(0, 3)
        x_out(5, 1)
        next1(1, 2, 1)
        x_out(6, 1)
        prod2(1, 2, 1)
        next1(1, 2, 2)
        q_wd(0)
        tr2(0, 0)
        prod2(3, 1, 1)
        next1(1, 2, 3)
        fin1(1, 2)
        x_out(4, 1)
        q_wd(1)
        prod2(1, 0, 1)
        q_x(1, 0)
        mm1(0, 0)
        ev2(0, 0)
        ev2(0, 1)
        mm1(0, 2)
        gelu(0, 0)
        q_wu(0)
        mm1(0, 3)
        gelu(0, 2)
        q_x(1, 1)
        mm1(0, 1)
        gelu(0, 3)
        ev2(2, 1)
        gelu(0, 1)
        mm1(1, 1)
        q_wu(2)
        u_mul(0, 0)
        mm1(1, 2)
        gelu(1, 1)
        mm1(1, 3)
        gelu(1, 2)
        mm1(1, 0)
        q_u(0, 0)
        gelu(1, 3)
        u_mul(0, 1)
        mm2(0, 2, 0)
        gelu(1, 0)
        mm2(0, 0, 0)
        tr2(1, 0)
        out_copy(0, 2, 0, 1)
        q_u(0, 1)
        out_copy(0, 0, 0, 1)
        u_mul(1, 1)
        mm2(0, 0, 1)
        mm2(0, 2, 1)
        ev2(1, 0)
        out_copy(0, 0, 1, 1)
        tr2(3, 1)
        out_copy(0, 2, 1, 0)
        cast_out(0, 0, 1)
        store_out(0, 0)
        q_u(1, 1)
        u_mul(1, 0)
        mm2(1, 0, 1)
        cast_out(0, 2, 1)
        store_out(0, 2)
        mm2(1, 2, 1)
        tr2(3, 0)
        q_out(0, 0)
        q_u(1, 0)
        out_copy(1, 0, 1, 1)
        q_out(0, 2)
        ev2(3, 1)
        out_copy(1, 2, 1, 1)
        mm2(1, 0, 0)
        ev2(3, 0)
        mm2(1, 2, 0)
        out_copy(1, 0, 0, 1)
        tr2(1, 1)
        q_wu(3)
        out_copy(1, 2, 0, 1)
        store_out(1, 0)
        cast_out(1, 0, 0)
        cast_out(1, 2, 1)
        q_out(1, 0)
        mm2(1, 3, 0)
        store_out(1, 2)
        ev2(1, 1)
        mm2(1, 3, 1)
        mm2(0, 3, 0)
        out_copy(1, 3, 1, 1)
        q_out(1, 2)
        mm2(0, 3, 1)
        out_copy(1, 3, 0, 0)
        out_copy(0, 3, 1, 1)
        q_wu(1)
        out_copy(0, 3, 0, 1)
        store_out(1, 3)
        cast_out(1, 3, 0)
        mm2(1, 1, 0)
        mm2(0, 1, 0)
        cast_out(0, 3, 1)
        mm2(1, 1, 1)
        q_out(1, 3)
        mm2(0, 1, 1)
        store_out(0, 3)
        out_copy(0, 1, 0, 0)
        out_copy(1, 1, 1, 1)
        q_out(0, 3)
        out_copy(0, 1, 1, 0)
        out_copy(1, 1, 0, 0)
        cast_out(0, 1, 1)
        store_out(0, 1)
        cast_out(1, 1, 0)
        store_out(1, 1)
        q_out(1, 1)
        q_out(0, 1)
        for h in range(2):
            store_scales(h)
